import numpy as np
import ml_dtypes

BF16 = ml_dtypes.bfloat16


def bf(x):
    return np.asarray(x, np.float32).astype(BF16)


def f32(x):
    return np.asarray(x, np.float32)


def f64(x):
    return np.asarray(x).astype(np.float64)


def striped(idx):
    return np.concatenate([l.reshape(-1, 16).T for l in idx])


def rows(idx, k):
    return np.tile(np.repeat(idx, 16, axis=0), (k // (16 * 8), 1))


def look(tab, idx):
    return np.take_along_axis(f64(tab), rows(idx, len(tab)), axis=1)


K, S, V, N, M = 256, 2048, 1024, 1024, 128


def setup_inputs():
    return {"tab": f32(np.random.standard_normal((K, S))), "w": bf(np.random.standard_normal((K, M)) / np.sqrt(K)), "b": f32(0.5 * np.random.standard_normal((M, 1))), "offs": striped(np.random.randint(0, S, (8, N)))}


def reference(tab, w, b, offs):
    idx = np.stack([g.T.reshape(-1) for g in np.split(offs, 8)])
    t = look(tab, idx)
    x = 0.75 * t + 0.25
    y = f64(w).T @ x
    return np.maximum(y + f64(b), 0.0)

import concourse.mybir as mybir

K, S, N, M = 256, 2048, 1024, 128
P = 128
BLOCKS = K // P
PIECE = 512
PIECES = N // PIECE
STRIPE = 16
SCALE, SHIFT = 0.75, 0.25

FLOPS = 2 * K * M * N

BF16, F32, U16 = mybir.dt.bfloat16, mybir.dt.float32, mybir.dt.uint16
MULT, ADD = mybir.AluOpType.mult, mybir.AluOpType.add
RELU = mybir.ActivationFunctionType.Relu


def tile_lookup_deq_aff_relu_kernel(tc, tab, w, b, offs, out):
    nc = tc.nc
    with (
        tc.tile_pool(name="held", bufs=1) as held,
        tc.psum_pool(name="psum", bufs=1) as psum,
    ):
        offsets = held.tile([P, N // STRIPE], U16, name="offsets")
        windows = [held.tile([P, S], F32, name=f"window{r}") for r in range(BLOCKS)]
        weights = held.tile([P, BLOCKS, M], BF16, name="weights")
        bias = held.tile([M, 1], F32, name="bias")

        nc.sync.dma_start(offsets[:], offs)
        for r in range(BLOCKS):
            nc.sync.dma_start(windows[r][:], tab[r * P : (r + 1) * P, :])
        nc.scalar.dma_start(weights[:], w.rearrange("(r p) m -> p r m", p=P))
        nc.scalar.dma_start(bias[:], b)

        banks = [psum.tile([M, PIECE], F32, name=f"bank{c}") for c in range(PIECES)]
        for r in range(BLOCKS):
            for c in range(PIECES):
                codes = offsets[:, c * PIECE // STRIPE : (c + 1) * PIECE // STRIPE]
                x = held.tile([P, PIECE], BF16, name=f"x{r}_{c}")
                nc.vector.tensor_scalar(x[:], windows[r][:].indirect(codes), SCALE, SHIFT, MULT, ADD)
                nc.tensor.matmul(banks[c][:], weights[:, r, :], x[:], start=(r == 0), stop=(r == BLOCKS - 1))

        for c in range(PIECES):
            y = held.tile([M, PIECE], F32, name=f"y{c}")
            nc.scalar.activation(y[:], banks[c][:], RELU, bias=bias[:])
            nc.sync.dma_start(out[:, c * PIECE : (c + 1) * PIECE], y[:])
